import numpy as np
import ml_dtypes


def mxq(x, axis, fmt="e4m3"):
    dtype, down = {"e4m3": (ml_dtypes.float8_e4m3fn, 7), "e5m2": (ml_dtypes.float8_e5m2, 14)}[fmt]
    v = np.moveaxis(np.asarray(x, np.float32).astype(ml_dtypes.bfloat16).astype(np.float64), axis, -1)
    blocks = v.reshape(v.shape[:-1] + (-1, 32))
    amax = np.abs(blocks).max(-1, keepdims=True)
    byte = np.maximum(np.where(amax > 0, np.frexp(amax)[1] - 1 + 127, 0) - down, 1)
    scale = np.exp2(byte - 127.0)
    codes = (blocks / scale).astype(np.float32).astype(dtype).astype(np.float64)
    return np.moveaxis((codes * scale).reshape(v.shape), -1, axis)


WIDE = False


def mx_kscale(k, group=512):
    if not WIDE:
        return np.ones(k)
    levels = np.array([10, -10, 5, -5, 0])
    if group != 512:
        return np.exp2(np.random.permutation(np.resize(levels, k // group))).repeat(group)
    if k % 512:
        return np.exp2(np.random.permutation(np.resize(levels, k // 32))).repeat(32)
    a = np.empty((k // 512, 16))
    for p in range(k // 512):
        a[p, :8] = np.random.permutation(np.resize(levels, 8))
        for g in range(8):
            far = levels[np.abs(levels - a[p, g]) >= 10]
            a[p, g + 8] = far[np.random.randint(len(far))]
    return np.exp2(a.ravel()).repeat(32)


def f64(x):
    return np.asarray(x).astype(np.float64)


E2M1 = np.array([0.0, 0.5, 1.0, 1.5, 2.0, 3.0, 4.0, 6.0, -0.0, -0.5, -1.0, -1.5, -2.0, -3.0, -4.0, -6.0])


def pack_group(w):
    k, n = w.shape
    w = f64(np.asarray(w, np.float32).astype(ml_dtypes.bfloat16)).reshape(k // 32, 32, n)
    amax = np.abs(w).max(1)
    mant, ex = np.frexp(amax / 6.0)
    byte = np.clip(np.where(amax > 0, np.where(mant > 0.5, ex, ex - 1) + 127, 1), 1, 254)
    scaled = (w * np.exp2(127.0 - byte)[:, None, :]).reshape(k, n).astype(np.float32)
    c = np.ascontiguousarray(scaled.reshape(k // 4, 4, n).transpose(0, 2, 1)).astype(ml_dtypes.float4_e2m1fn).view(np.uint8) & 0xF
    return np.ascontiguousarray((c[..., 0::2] | (c[..., 1::2] << 4)).reshape(k // 4, 2 * n)), byte.astype(np.uint8)


def unpack_group(words, scales):
    p, n = words.shape[0], scales.shape[1]
    words = np.ascontiguousarray(words).reshape(p, n, 2)
    nib = np.empty((p, n, 4), np.uint8)
    nib[..., 0::2] = words & 0xF
    nib[..., 1::2] = words >> 4
    return E2M1[nib].transpose(0, 2, 1).reshape(4 * p, n) * np.repeat(np.exp2(scales.astype(np.float64) - 127.0), 32, axis=0)


G, D, M, N = 4, 256, 128, 1024


def setup_inputs():
    n = np.random.standard_normal
    s = mx_kscale(D, 0)[:, None]
    w_ = [pack_group(w) for w in n((G, D, M)) / np.sqrt(D) / s]
    u_ = [pack_group(w) for w in n((G, D, M)) / np.sqrt(D) / s]
    return {
        "x": (n((G, D, N)) * s).astype(np.float32),
        "w_words": np.stack([w[0] for w in w_]),
        "w_scales": np.stack([w[1] for w in w_]),
        "u_words": np.stack([w[0] for w in u_]),
        "u_scales": np.stack([w[1] for w in u_]),
        "b": (0.5 * n((G, M, 1))).astype(np.float32),
    }


def reference(x, w_words, w_scales, u_words, u_scales, b):
    xq = mxq(f64(x), 1, "e4m3")
    h = np.stack([unpack_group(w_words[g], w_scales[g]) for g in range(G)]).transpose(0, 2, 1) @ xq
    g = np.stack([unpack_group(u_words[g], u_scales[g]) for g in range(G)]).transpose(0, 2, 1) @ xq
    h = h + f64(b)
    y = np.maximum(h, 0.0) * g
    return y

@@ -1,0 +1,165 @@
+from contextlib import ExitStack
+
+import concourse.mybir as mybir
+
+G, D, M, N = 4, 256, 128, 1024
+FLOPS = 2 * 2 * G * D * M * N
+
+F32 = mybir.dt.float32
+BF16 = mybir.dt.bfloat16
+I32 = mybir.dt.int32
+U32 = mybir.dt.uint32
+U8 = mybir.dt.uint8
+FP8X4 = mybir.dt.float8_e4m3fn_x4
+FP4X4 = mybir.dt.float4_e2m1fn_x4
+RELU = mybir.ActivationFunctionType.Relu
+MULT = mybir.AluOpType.mult
+
+P = 128
+PACK = 4
+ROWS = D // PACK
+SIDE = P // ROWS
+PAIRS = G // SIDE
+PASS_N = 512
+
+PIECES = [
+    (0, 0, 256, 96),
+    (0, 256, 256, 96),
+    (0, 512, 512, 192),
+    (1, 0, 512, 192),
+    (1, 512, 256, 96),
+    (1, 768, 256, 96),
+]
+UNITS = [(0, 0, 512), (0, 512, 512), (1, 0, 512), (1, 512, 256), (1, 768, 256)]
+
+
+def tile_rows_gglu_relu_bias_kernel(tc, x, w_words, w_scales, u_words, u_scales, b, out):
+    nc = tc.nc
+    with ExitStack() as ctx:
+        keep = ctx.enter_context(tc.tile_pool(name="keep", bufs=1))
+        psum = ctx.enter_context(tc.psum_pool(name="psum", bufs=1))
+        ctx.enter_context(tc.manual_schedule())
+
+        words = keep.tile([P, 2, PAIRS, 2 * M], U8, align_bytes=64, name="words")
+        wsc = keep.tile([P, 2, PAIRS, M], U8, align_bytes=64, name="wsc")
+        bias = keep.tile([P, G], F32, name="bias")
+        warm = keep.tile([P, 8], F32, name="warm")
+        warm2 = keep.tile([P, 8], F32, name="warm2")
+        raw = [keep.tile([P, PACK, w], F32, align_bytes=64, name="raw%d" % i) for i, (q, c0, w, s) in enumerate(PIECES)]
+        packed = [keep.tile([P, w, PACK], BF16, align_bytes=64, name="packed%d" % i) for i, (q, c0, w, s) in enumerate(PIECES)]
+        codes = [keep.tile([P, N], U32, align_bytes=64, name="codes%d" % q) for q in range(PAIRS)]
+        xsc = [keep.tile([P, N], U8, align_bytes=64, name="xsc%d" % q) for q in range(PAIRS)]
+        gate = [keep.tile([P, SIDE, N], F32, align_bytes=64, name="gate%d" % q) for q in range(PAIRS)]
+        res = [keep.tile([P, SIDE, N], F32, align_bytes=64, name="res%d" % q) for q in range(PAIRS)]
+        banks = {}
+        for c in range(SIDE):
+            for t in range(2):
+                for slot in range(2):
+                    banks[(c, t, slot)] = psum.tile([M, PASS_N], F32, name="bank%d%d%d" % (c, t, slot))
+
+        xv = x.rearrange("(q c) (p j) n -> q (c p) j n", c=SIDE, j=PACK)
+        ov = out.rearrange("(q c) m n -> q m c n", c=SIDE)
+
+        def load_x(i):
+            q, c0, w, s = PIECES[i]
+            nc.sync.dma_start(out=raw[i][:], in_=xv[q, :, :, c0 : c0 + w])
+
+        def load_scales(t, quad, eng):
+            src = (w_scales, u_scales)[t].rearrange("(q c) (h l) m -> (c h) l q m", c=SIDE, l=4)
+            eng.dma_start(out=wsc[32 * quad : 32 * quad + 4, t, :, :].bitcast(I32), in_=src[quad].bitcast(I32))
+
+        def load_words(t):
+            src = (w_words, u_words)[t].rearrange("(q c) p y -> (c p) q y", c=SIDE)
+            nc.gpsimd.dma_start(out=words[:, t, :, :].bitcast(I32), in_=src.bitcast(I32))
+
+        def interleave(eng, i):
+            q, c0, w, s = PIECES[i]
+            cols = slice(0, s) if eng == "s" else slice(s, w)
+            dst = packed[i][:, cols, :]
+            src = raw[i][:, :, cols].rearrange("p j n -> p n j")
+            if eng == "s":
+                nc.scalar.copy(out=dst, in_=src)
+            else:
+                nc.vector.tensor_copy(out=dst, in_=src)
+
+        def quantise(i):
+            q, c0, w, s = PIECES[i]
+            nc.vector.quantize_mx(
+                out=codes[q][:, c0 : c0 + w].bitcast(FP8X4),
+                scales=xsc[q][:, c0 : c0 + w],
+                in_=packed[i][:].rearrange("p n j -> p (n j)"),
+            )
+
+        def multiply(u):
+            q, c0, w = UNITS[u]
+            win = slice(c0 + w - PASS_N, c0 + w)
+            for t in range(2):
+                for c in range(SIDE):
+                    rows = slice(ROWS * c, ROWS * (c + 1))
+                    nc.tensor.matmul_mx(
+                        out=banks[(c, t, u % 2)][:],
+                        lhsT=words[rows, t, q, :].bitcast(FP4X4),
+                        lhsT_scale=wsc[rows, t, q, :],
+                        rhs=codes[q][rows, win].bitcast(FP8X4),
+                        rhs_scale=xsc[q][rows, win],
+                        start=True,
+                        stop=True,
+                    )
+
+        def relu(u, c):
+            q, c0, w = UNITS[u]
+            g = SIDE * q + c
+            nc.scalar.activation(
+                out=gate[q][:, c, c0 : c0 + w], in_=banks[(c, 0, u % 2)][:, PASS_N - w :], func=RELU, bias=bias[:, g : g + 1]
+            )
+
+        def product(u, c):
+            q, c0, w = UNITS[u]
+            nc.vector.tensor_tensor(
+                out=res[q][:, c, c0 : c0 + w], in0=banks[(c, 1, u % 2)][:, PASS_N - w :], in1=gate[q][:, c, c0 : c0 + w], op=MULT
+            )
+
+        def store(q, c0, w):
+            nc.sync.dma_start(out=ov[q, :, :, c0 : c0 + w], in_=res[q][:, :, c0 : c0 + w])
+
+        nc.vector.memset(wsc[:].rearrange("p t q m -> p (t q m)").bitcast(I32), 0)
+        nc.vector.memset(warm[:], 0.0)
+        load_words(0)
+        load_words(1)
+        load_scales(1, 3, nc.gpsimd)
+        for quad in range(3):
+            load_scales(0, quad, nc.scalar)
+        for i in range(3):
+            load_x(i)
+        load_scales(0, 3, nc.scalar)
+        load_scales(1, 0, nc.scalar)
+        nc.scalar.activation(out=warm2[:], in_=warm[:], func=RELU)
+        for quad in range(1, 3):
+            load_scales(1, quad, nc.scalar)
+        with nc.allow_non_contiguous_dma(reason="one bias a partition"):
+            nc.scalar.dma_start(out=bias[:], in_=b.rearrange("g m o -> m (g o)"))
+        for i in range(3, 6):
+            load_x(i)
+
+        for i in range(2):
+            interleave("s", i)
+            interleave("v", i)
+            quantise(i)
+        multiply(0)
+        for u in range(len(UNITS) - 1):
+            relu(u, 0)
+            interleave("s", u + 2)
+            interleave("v", u + 2)
+            relu(u, 1)
+            product(u, 0)
+            quantise(u + 2)
+            multiply(u + 1)
+            product(u, 1)
+        u = len(UNITS) - 1
+        for c in range(SIDE):
+            relu(u, c)
+            product(u, c)
+        store(0, 0, 1024)
+        store(1, 0, 512)
+        store(1, 512, 256)
+        store(1, 768, 256)

@@ -14,6 +14,7 @@ FP8X4 = mybir.dt.float8_e4m3fn_x4
 FP4X4 = mybir.dt.float4_e2m1fn_x4
 RELU = mybir.ActivationFunctionType.Relu
 MULT = mybir.AluOpType.mult
+ADD = mybir.AluOpType.add
 
 P = 128
 PACK = 4
@@ -22,15 +23,10 @@ SIDE = P // ROWS
 PAIRS = G // SIDE
 PASS_N = 512
 
-PIECES = [
-    (0, 0, 256, 96),
-    (0, 256, 256, 96),
-    (0, 512, 512, 192),
-    (1, 0, 512, 192),
-    (1, 512, 256, 96),
-    (1, 768, 256, 96),
-]
-UNITS = [(0, 0, 512), (0, 512, 512), (1, 0, 512), (1, 512, 256), (1, 768, 256)]
+PIECES = [(0,0,256,96,0),(0,256,256,96,0),(0,512,256,96,0),(0,768,256,64,0),(1,0,256,208,0),(1,256,256,32,0),(1,512,256,192,0),(1,768,256,80,0)]
+UNITS = [(0,0,512),(0,512,512),(1,0,512),(1,512,512)]
+LOADS = "sw0 sx0 ss00 ss01 ss02 ss03 sb sx1 sx2 sw1 ss10 ss11 ss12 ss13 sx3 sx4 sx5 sx6 sx7"
+ORDER = "S0 V0 q0 S1 V1 q1 P0 S2 V2 q2 r00 S3 V3 m00 r01 q3 P1 V4 S4 m01 V5 S5 q45 P2 r10 m10 S6 V6 S7 V7 q67 r11 m11 P3 r20 m20 r21 m21 r30 m30 r31 h310 h311"
 
 
 def tile_rows_gglu_relu_bias_kernel(tc, x, w_words, w_scales, u_words, u_scales, b, out):
@@ -45,12 +41,12 @@ def tile_rows_gglu_relu_bias_kernel(tc, x, w_words, w_scales, u_words, u_scales,
         bias = keep.tile([P, G], F32, name="bias")
         warm = keep.tile([P, 8], F32, name="warm")
         warm2 = keep.tile([P, 8], F32, name="warm2")
-        raw = [keep.tile([P, PACK, w], F32, align_bytes=64, name="raw%d" % i) for i, (q, c0, w, s) in enumerate(PIECES)]
-        packed = [keep.tile([P, w, PACK], BF16, align_bytes=64, name="packed%d" % i) for i, (q, c0, w, s) in enumerate(PIECES)]
-        codes = [keep.tile([P, N], U32, align_bytes=64, name="codes%d" % q) for q in range(PAIRS)]
-        xsc = [keep.tile([P, N], U8, align_bytes=64, name="xsc%d" % q) for q in range(PAIRS)]
-        gate = [keep.tile([P, SIDE, N], F32, align_bytes=64, name="gate%d" % q) for q in range(PAIRS)]
-        res = [keep.tile([P, SIDE, N], F32, align_bytes=64, name="res%d" % q) for q in range(PAIRS)]
+        raw = [keep.tile([P, PACK, pc[2]], F32, align_bytes=256, name="raw%d" % i) for i, pc in enumerate(PIECES)]
+        packed = keep.tile([P, PAIRS * N, PACK], BF16, align_bytes=256, name="packed")
+        codes = keep.tile([P, PAIRS * N], U32, align_bytes=256, name="codes")
+        xsc = keep.tile([P, PAIRS * N], U8, align_bytes=256, name="xsc")
+        gate = [keep.tile([P, SIDE, N], F32, align_bytes=256, name="gate%d" % q) for q in range(PAIRS)]
+        res = [keep.tile([P, SIDE, N], F32, align_bytes=256, name="res%d" % q) for q in range(PAIRS)]
         banks = {}
         for c in range(SIDE):
             for t in range(2):
@@ -58,53 +54,66 @@ def tile_rows_gglu_relu_bias_kernel(tc, x, w_words, w_scales, u_words, u_scales,
                     banks[(c, t, slot)] = psum.tile([M, PASS_N], F32, name="bank%d%d%d" % (c, t, slot))
 
         xv = x.rearrange("(q c) (p j) n -> q (c p) j n", c=SIDE, j=PACK)
-        ov = out.rearrange("(q c) m n -> q m c n", c=SIDE)
+        queues = {"s": nc.sync, "a": nc.scalar, "g": nc.gpsimd}
 
-        def load_x(i):
-            q, c0, w, s = PIECES[i]
-            nc.sync.dma_start(out=raw[i][:], in_=xv[q, :, :, c0 : c0 + w])
-
-        def load_scales(t, quad, eng):
-            src = (w_scales, u_scales)[t].rearrange("(q c) (h l) m -> (c h) l q m", c=SIDE, l=4)
-            eng.dma_start(out=wsc[32 * quad : 32 * quad + 4, t, :, :].bitcast(I32), in_=src[quad].bitcast(I32))
-
-        def load_words(t):
-            src = (w_words, u_words)[t].rearrange("(q c) p y -> (c p) q y", c=SIDE)
-            nc.gpsimd.dma_start(out=words[:, t, :, :].bitcast(I32), in_=src.bitcast(I32))
+        def load(name):
+            eng, kind, arg = queues[name[0]], name[1], name[2:]
+            if kind == "x":
+                i = int(arg)
+                q, c0, w, s, gp = PIECES[i]
+                eng.dma_start(out=raw[i][:], in_=xv[q, :, :, c0 : c0 + w])
+            elif kind == "s":
+                t, quad = int(arg[0]), int(arg[1])
+                src = (w_scales, u_scales)[t].rearrange("(q c) (h l) m -> (c h) l q m", c=SIDE, l=4)
+                eng.dma_start(out=wsc[32 * quad : 32 * quad + 4, t, :, :].bitcast(I32), in_=src[quad].bitcast(I32))
+            elif kind == "w":
+                t = int(arg)
+                src = (w_words, u_words)[t].rearrange("(q c) p y -> (c p) q y", c=SIDE)
+                eng.dma_start(out=words[:, t, :, :].bitcast(I32), in_=src.bitcast(I32))
+            else:
+                with nc.allow_non_contiguous_dma(reason="one bias a partition"):
+                    eng.dma_start(out=bias[:], in_=b.rearrange("g m o -> m (g o)"))
 
         def interleave(eng, i):
-            q, c0, w, s = PIECES[i]
-            cols = slice(0, s) if eng == "s" else slice(s, w)
-            dst = packed[i][:, cols, :]
-            src = raw[i][:, :, cols].rearrange("p j n -> p n j")
-            if eng == "s":
-                nc.scalar.copy(out=dst, in_=src)
+            q, c0, w, s, gp = PIECES[i]
+            lo, hi = {"S": (0, s), "G": (s, s + gp), "V": (s + gp, w)}[eng]
+            base = q * N + c0
+            dst = packed[:, base + lo : base + hi, :]
+            src = raw[i][:, :, lo:hi]
+            if eng in "-":
+                dst = dst.rearrange("p (c i) j -> p c j i", i=4)
+                src = src.rearrange("p j (c i) -> p c j i", i=4)
             else:
+                src = src.rearrange("p j n -> p n j")
+            if eng == "S":
+                nc.scalar.copy(out=dst, in_=src)
+            elif eng == "V":
                 nc.vector.tensor_copy(out=dst, in_=src)
+            else:
+                nc.gpsimd.tensor_scalar(out=dst, in0=src, scalar1=1.0, scalar2=0.0, op0=MULT, op1=ADD)
 
-        def quantise(i):
-            q, c0, w, s = PIECES[i]
+        def quantise(i, last):
+            lo = PIECES[i][0] * N + PIECES[i][1]
+            hi = PIECES[last][0] * N + PIECES[last][1] + PIECES[last][2]
             nc.vector.quantize_mx(
-                out=codes[q][:, c0 : c0 + w].bitcast(FP8X4),
-                scales=xsc[q][:, c0 : c0 + w],
-                in_=packed[i][:].rearrange("p n j -> p (n j)"),
+                out=codes[:, lo:hi].bitcast(FP8X4),
+                scales=xsc[:, lo:hi],
+                in_=packed[:, lo:hi, :].rearrange("p n j -> p (n j)"),
             )
 
-        def multiply(u):
+        def multiply(u, t, c):
             q, c0, w = UNITS[u]
-            win = slice(c0 + w - PASS_N, c0 + w)
-            for t in range(2):
-                for c in range(SIDE):
-                    rows = slice(ROWS * c, ROWS * (c + 1))
-                    nc.tensor.matmul_mx(
-                        out=banks[(c, t, u % 2)][:],
-                        lhsT=words[rows, t, q, :].bitcast(FP4X4),
-                        lhsT_scale=wsc[rows, t, q, :],
-                        rhs=codes[q][rows, win].bitcast(FP8X4),
-                        rhs_scale=xsc[q][rows, win],
-                        start=True,
-                        stop=True,
-                    )
+            win = slice(q * N + c0 + w - PASS_N, q * N + c0 + w)
+            rows = slice(ROWS * c, ROWS * (c + 1))
+            nc.tensor.matmul_mx(
+                out=banks[(c, t, u % 2)][:],
+                lhsT=words[rows, t, q, :].bitcast(FP4X4),
+                lhsT_scale=wsc[rows, t, q, :],
+                rhs=codes[rows, win].bitcast(FP8X4),
+                rhs_scale=xsc[rows, win],
+                start=True,
+                stop=True,
+            )
 
         def relu(u, c):
             q, c0, w = UNITS[u]
@@ -113,53 +122,38 @@ def tile_rows_gglu_relu_bias_kernel(tc, x, w_words, w_scales, u_words, u_scales,
                 out=gate[q][:, c, c0 : c0 + w], in_=banks[(c, 0, u % 2)][:, PASS_N - w :], func=RELU, bias=bias[:, g : g + 1]
             )
 
-        def product(u, c):
+        def product(u, c, lo, hi):
             q, c0, w = UNITS[u]
+            cols = slice(c0 + lo, c0 + hi)
             nc.vector.tensor_tensor(
-                out=res[q][:, c, c0 : c0 + w], in0=banks[(c, 1, u % 2)][:, PASS_N - w :], in1=gate[q][:, c, c0 : c0 + w], op=MULT
+                out=res[q][:, c, cols], in0=banks[(c, 1, u % 2)][:, PASS_N - w + lo : PASS_N - w + hi], in1=gate[q][:, c, cols], op=MULT
             )
-
-        def store(q, c0, w):
-            nc.sync.dma_start(out=ov[q, :, :, c0 : c0 + w], in_=res[q][:, :, c0 : c0 + w])
+            nc.sync.dma_start(out=out[SIDE * q + c, :, cols], in_=res[q][:, c, cols])
 
         nc.vector.memset(wsc[:].rearrange("p t q m -> p (t q m)").bitcast(I32), 0)
         nc.vector.memset(warm[:], 0.0)
-        load_words(0)
-        load_words(1)
-        load_scales(1, 3, nc.gpsimd)
-        for quad in range(3):
-            load_scales(0, quad, nc.scalar)
-        for i in range(3):
-            load_x(i)
-        load_scales(0, 3, nc.scalar)
-        load_scales(1, 0, nc.scalar)
         nc.scalar.activation(out=warm2[:], in_=warm[:], func=RELU)
-        for quad in range(1, 3):
-            load_scales(1, quad, nc.scalar)
-        with nc.allow_non_contiguous_dma(reason="one bias a partition"):
-            nc.scalar.dma_start(out=bias[:], in_=b.rearrange("g m o -> m (g o)"))
-        for i in range(3, 6):
-            load_x(i)
-
-        for i in range(2):
-            interleave("s", i)
-            interleave("v", i)
-            quantise(i)
-        multiply(0)
-        for u in range(len(UNITS) - 1):
-            relu(u, 0)
-            interleave("s", u + 2)
-            interleave("v", u + 2)
-            relu(u, 1)
-            product(u, 0)
-            quantise(u + 2)
-            multiply(u + 1)
-            product(u, 1)
-        u = len(UNITS) - 1
-        for c in range(SIDE):
-            relu(u, c)
-            product(u, c)
-        store(0, 0, 1024)
-        store(1, 0, 512)
-        store(1, 512, 256)
-        store(1, 768, 256)
+        for name in LOADS.split():
+            if name == "warm":
+                nc.scalar.activation(out=warm2[:], in_=warm[:], func=RELU)
+            else:
+                load(name)
+        for step in ORDER.split():
+            kind, arg = step[0], step[1:]
+            if kind in "SVG":
+                interleave(kind, int(arg))
+            elif kind == "q":
+                quantise(int(arg[0]), int(arg[-1]))
+            elif kind == "P":
+                for t in range(2):
+                    for c in range(SIDE):
+                        multiply(int(arg), t, c)
+            elif kind == "p":
+                multiply(int(arg[0]), int(arg[1]), int(arg[2]))
+            elif kind == "r":
+                relu(int(arg[0]), int(arg[1]))
+            elif kind == "m":
+                product(int(arg[0]), int(arg[1]), 0, UNITS[int(arg[0])][2])
+            else:
+                half = UNITS[int(arg[0])][2] // 2
+                product(int(arg[0]), int(arg[1]), half * int(arg[2]), half * (int(arg[2]) + 1))

@@ -23,10 +23,10 @@ SIDE = P // ROWS
 PAIRS = G // SIDE
 PASS_N = 512
 
-PIECES = [(0,0,256,96,0),(0,256,256,96,0),(0,512,256,96,0),(0,768,256,64,0),(1,0,256,208,0),(1,256,256,32,0),(1,512,256,192,0),(1,768,256,80,0)]
-UNITS = [(0,0,512),(0,512,512),(1,0,512),(1,512,512)]
+PIECES = [(0,0,256,160,0),(0,256,256,80,0),(0,512,256,96,0),(0,768,256,64,0),(1,0,256,256,0),(1,256,256,112,0),(1,512,256,128,0),(1,768,256,128,0)]
+UNITS = [(0,0,512),(0,512,256),(0,768,256),(1,0,256),(1,256,256),(1,512,256),(1,768,256)]
 LOADS = "sw0 sx0 ss00 ss01 ss02 ss03 sb sx1 sx2 sw1 ss10 ss11 ss12 ss13 sx3 sx4 sx5 sx6 sx7"
-ORDER = "S0 V0 q0 S1 V1 q1 P0 S2 V2 q2 r00 S3 V3 m00 r01 q3 P1 V4 S4 m01 V5 S5 q45 P2 r10 m10 S6 V6 S7 V7 q67 r11 m11 P3 r20 m20 r21 m21 r30 m30 r31 h310 h311"
+ORDER = "S0 V0 q0 S1 V1 q1 P0 T0 S2 V2 q2 P1 r00 r01 S3 V3 m00 m01 q3 P2 r10 r11 m10 m11 S4 S5 V5 q4 P3 r20 r21 q5 m20 S6 V6 m21 P4 q6 r30 r31 m30 S7 V7 m31 P5 q7 r40 r41 m40 m41 P6 r50 r51 m50 m51 r60 r61 m60 m61"
 
 
 def tile_rows_gglu_relu_bias_kernel(tc, x, w_words, w_scales, u_words, u_scales, b, out):
@@ -38,7 +38,8 @@ def tile_rows_gglu_relu_bias_kernel(tc, x, w_words, w_scales, u_words, u_scales,
 
         words = keep.tile([P, 2, PAIRS, 2 * M], U8, align_bytes=64, name="words")
         wsc = keep.tile([P, 2, PAIRS, M], U8, align_bytes=64, name="wsc")
-        bias = keep.tile([P, G], F32, name="bias")
+        bias_rows = keep.tile([P, G * 32], F32, align_bytes=64, name="bias_rows")
+        bias = keep.tile([P, G * 32], F32, align_bytes=64, name="bias")
         warm = keep.tile([P, 8], F32, name="warm")
         warm2 = keep.tile([P, 8], F32, name="warm2")
         raw = [keep.tile([P, PACK, pc[2]], F32, align_bytes=256, name="raw%d" % i) for i, pc in enumerate(PIECES)]
@@ -71,8 +72,8 @@ def tile_rows_gglu_relu_bias_kernel(tc, x, w_words, w_scales, u_words, u_scales,
                 src = (w_words, u_words)[t].rearrange("(q c) p y -> (c p) q y", c=SIDE)
                 eng.dma_start(out=words[:, t, :, :].bitcast(I32), in_=src.bitcast(I32))
             else:
-                with nc.allow_non_contiguous_dma(reason="one bias a partition"):
-                    eng.dma_start(out=bias[:], in_=b.rearrange("g m o -> m (g o)"))
+                dst = bias_rows[0:P:32, :].rearrange("h (g i) -> h g i", g=G)
+                eng.dma_start(out=dst, in_=b.rearrange("g (h i) o -> h g (i o)", i=32))
 
         def interleave(eng, i):
             q, c0, w, s, gp = PIECES[i]
@@ -80,7 +81,7 @@ def tile_rows_gglu_relu_bias_kernel(tc, x, w_words, w_scales, u_words, u_scales,
             base = q * N + c0
             dst = packed[:, base + lo : base + hi, :]
             src = raw[i][:, :, lo:hi]
-            if eng in "-":
+            if eng in "VS-":
                 dst = dst.rearrange("p (c i) j -> p c j i", i=4)
                 src = src.rearrange("p j (c i) -> p c j i", i=4)
             else:
@@ -119,7 +120,7 @@ def tile_rows_gglu_relu_bias_kernel(tc, x, w_words, w_scales, u_words, u_scales,
             q, c0, w = UNITS[u]
             g = SIDE * q + c
             nc.scalar.activation(
-                out=gate[q][:, c, c0 : c0 + w], in_=banks[(c, 0, u % 2)][:, PASS_N - w :], func=RELU, bias=bias[:, g : g + 1]
+                out=gate[q][:, c, c0 : c0 + w], in_=banks[(c, 0, u % 2)][:, PASS_N - w :], func=RELU, bias=bias[:, 32 * g : 32 * g + 1]
             )
 
         def product(u, c, lo, hi):
@@ -131,6 +132,7 @@ def tile_rows_gglu_relu_bias_kernel(tc, x, w_words, w_scales, u_words, u_scales,
             nc.sync.dma_start(out=out[SIDE * q + c, :, cols], in_=res[q][:, c, cols])
 
         nc.vector.memset(wsc[:].rearrange("p t q m -> p (t q m)").bitcast(I32), 0)
+        nc.vector.memset(bias_rows[:], 0.0)
         nc.vector.memset(warm[:], 0.0)
         nc.scalar.activation(out=warm2[:], in_=warm[:], func=RELU)
         for name in LOADS.split():
@@ -144,6 +146,8 @@ def tile_rows_gglu_relu_bias_kernel(tc, x, w_words, w_scales, u_words, u_scales,
                 interleave(kind, int(arg))
             elif kind == "q":
                 quantise(int(arg[0]), int(arg[-1]))
+            elif kind == "T":
+                nc.vector.transpose(out=bias[:], in_=bias_rows[:])
             elif kind == "P":
                 for t in range(2):
                     for c in range(SIDE):

from contextlib import ExitStack

import concourse.mybir as mybir

G, D, M, N = 4, 256, 128, 1024
FLOPS = 2 * 2 * G * D * M * N

F32 = mybir.dt.float32
BF16 = mybir.dt.bfloat16
I32 = mybir.dt.int32
U32 = mybir.dt.uint32
U8 = mybir.dt.uint8
FP8X4 = mybir.dt.float8_e4m3fn_x4
FP4X4 = mybir.dt.float4_e2m1fn_x4
RELU = mybir.ActivationFunctionType.Relu
MULT = mybir.AluOpType.mult
ADD = mybir.AluOpType.add

P = 128
PACK = 4
ROWS = D // PACK
SIDE = P // ROWS
PAIRS = G // SIDE
PASS_N = 512

PIECES = [(0,0,256,160,0),(0,256,256,80,0),(0,512,256,96,0),(0,768,256,64,0),(1,0,256,256,0),(1,256,256,112,0),(1,512,256,128,0),(1,768,256,128,0)]
UNITS = [(0,0,512),(0,512,256),(0,768,256),(1,0,256),(1,256,256),(1,512,256),(1,768,256)]
LOADS = "sw0 sx0 ss00 ss01 ss02 ss03 sb sx1 sx2 sw1 ss10 ss11 ss12 ss13 sx3 sx4 sx5 sx6 sx7"
ORDER = "S0 V0 q0 S1 V1 q1 P0 T0 S2 V2 q2 P1 r00 r01 S3 V3 m00 m01 q3 P2 r10 r11 m10 m11 S4 S5 V5 q4 P3 r20 r21 q5 m20 S6 V6 m21 P4 q6 r30 r31 m30 S7 V7 m31 P5 q7 r40 r41 m40 m41 P6 r50 r51 m50 m51 r60 r61 m60 m61"


def tile_rows_gglu_relu_bias_kernel(tc, x, w_words, w_scales, u_words, u_scales, b, out):
    nc = tc.nc
    with ExitStack() as ctx:
        keep = ctx.enter_context(tc.tile_pool(name="keep", bufs=1))
        psum = ctx.enter_context(tc.psum_pool(name="psum", bufs=1))
        ctx.enter_context(tc.manual_schedule())

        words = keep.tile([P, 2, PAIRS, 2 * M], U8, align_bytes=64, name="words")
        wsc = keep.tile([P, 2, PAIRS, M], U8, align_bytes=64, name="wsc")
        bias_rows = keep.tile([P, G * 32], F32, align_bytes=64, name="bias_rows")
        bias = keep.tile([P, G * 32], F32, align_bytes=64, name="bias")
        warm = keep.tile([P, 8], F32, name="warm")
        warm2 = keep.tile([P, 8], F32, name="warm2")
        raw = [keep.tile([P, PACK, pc[2]], F32, align_bytes=256, name="raw%d" % i) for i, pc in enumerate(PIECES)]
        packed = keep.tile([P, PAIRS * N, PACK], BF16, align_bytes=256, name="packed")
        codes = keep.tile([P, PAIRS * N], U32, align_bytes=256, name="codes")
        xsc = keep.tile([P, PAIRS * N], U8, align_bytes=256, name="xsc")
        gate = [keep.tile([P, SIDE, N], F32, align_bytes=256, name="gate%d" % q) for q in range(PAIRS)]
        res = [keep.tile([P, SIDE, N], F32, align_bytes=256, name="res%d" % q) for q in range(PAIRS)]
        banks = {}
        for c in range(SIDE):
            for t in range(2):
                for slot in range(2):
                    banks[(c, t, slot)] = psum.tile([M, PASS_N], F32, name="bank%d%d%d" % (c, t, slot))

        xv = x.rearrange("(q c) (p j) n -> q (c p) j n", c=SIDE, j=PACK)
        queues = {"s": nc.sync, "a": nc.scalar, "g": nc.gpsimd}

        def load(name):
            eng, kind, arg = queues[name[0]], name[1], name[2:]
            if kind == "x":
                i = int(arg)
                q, c0, w, s, gp = PIECES[i]
                eng.dma_start(out=raw[i][:], in_=xv[q, :, :, c0 : c0 + w])
            elif kind == "s":
                t, quad = int(arg[0]), int(arg[1])
                src = (w_scales, u_scales)[t].rearrange("(q c) (h l) m -> (c h) l q m", c=SIDE, l=4)
                eng.dma_start(out=wsc[32 * quad : 32 * quad + 4, t, :, :].bitcast(I32), in_=src[quad].bitcast(I32))
            elif kind == "w":
                t = int(arg)
                src = (w_words, u_words)[t].rearrange("(q c) p y -> (c p) q y", c=SIDE)
                eng.dma_start(out=words[:, t, :, :].bitcast(I32), in_=src.bitcast(I32))
            else:
                dst = bias_rows[0:P:32, :].rearrange("h (g i) -> h g i", g=G)
                eng.dma_start(out=dst, in_=b.rearrange("g (h i) o -> h g (i o)", i=32))

        def interleave(eng, i):
            q, c0, w, s, gp = PIECES[i]
            lo, hi = {"S": (0, s), "G": (s, s + gp), "V": (s + gp, w)}[eng]
            base = q * N + c0
            dst = packed[:, base + lo : base + hi, :]
            src = raw[i][:, :, lo:hi]
            if eng in "VS-":
                dst = dst.rearrange("p (c i) j -> p c j i", i=4)
                src = src.rearrange("p j (c i) -> p c j i", i=4)
            else:
                src = src.rearrange("p j n -> p n j")
            if eng == "S":
                nc.scalar.copy(out=dst, in_=src)
            elif eng == "V":
                nc.vector.tensor_copy(out=dst, in_=src)
            else:
                nc.gpsimd.tensor_scalar(out=dst, in0=src, scalar1=1.0, scalar2=0.0, op0=MULT, op1=ADD)

        def quantise(i, last):
            lo = PIECES[i][0] * N + PIECES[i][1]
            hi = PIECES[last][0] * N + PIECES[last][1] + PIECES[last][2]
            nc.vector.quantize_mx(
                out=codes[:, lo:hi].bitcast(FP8X4),
                scales=xsc[:, lo:hi],
                in_=packed[:, lo:hi, :].rearrange("p n j -> p (n j)"),
            )

        def multiply(u, t, c):
            q, c0, w = UNITS[u]
            win = slice(q * N + c0 + w - PASS_N, q * N + c0 + w)
            rows = slice(ROWS * c, ROWS * (c + 1))
            nc.tensor.matmul_mx(
                out=banks[(c, t, u % 2)][:],
                lhsT=words[rows, t, q, :].bitcast(FP4X4),
                lhsT_scale=wsc[rows, t, q, :],
                rhs=codes[rows, win].bitcast(FP8X4),
                rhs_scale=xsc[rows, win],
                start=True,
                stop=True,
            )

        def relu(u, c):
            q, c0, w = UNITS[u]
            g = SIDE * q + c
            nc.scalar.activation(
                out=gate[q][:, c, c0 : c0 + w], in_=banks[(c, 0, u % 2)][:, PASS_N - w :], func=RELU, bias=bias[:, 32 * g : 32 * g + 1]
            )

        def product(u, c, lo, hi):
            q, c0, w = UNITS[u]
            cols = slice(c0 + lo, c0 + hi)
            nc.vector.tensor_tensor(
                out=res[q][:, c, cols], in0=banks[(c, 1, u % 2)][:, PASS_N - w + lo : PASS_N - w + hi], in1=gate[q][:, c, cols], op=MULT
            )
            nc.sync.dma_start(out=out[SIDE * q + c, :, cols], in_=res[q][:, c, cols])

        nc.vector.memset(wsc[:].rearrange("p t q m -> p (t q m)").bitcast(I32), 0)
        nc.vector.memset(bias_rows[:], 0.0)
        nc.vector.memset(warm[:], 0.0)
        nc.scalar.activation(out=warm2[:], in_=warm[:], func=RELU)
        for name in LOADS.split():
            if name == "warm":
                nc.scalar.activation(out=warm2[:], in_=warm[:], func=RELU)
            else:
                load(name)
        for step in ORDER.split():
            kind, arg = step[0], step[1:]
            if kind in "SVG":
                interleave(kind, int(arg))
            elif kind == "q":
                quantise(int(arg[0]), int(arg[-1]))
            elif kind == "T":
                nc.vector.transpose(out=bias[:], in_=bias_rows[:])
            elif kind == "P":
                for t in range(2):
                    for c in range(SIDE):
                        multiply(int(arg), t, c)
            elif kind == "p":
                multiply(int(arg[0]), int(arg[1]), int(arg[2]))
            elif kind == "r":
                relu(int(arg[0]), int(arg[1]))
            elif kind == "m":
                product(int(arg[0]), int(arg[1]), 0, UNITS[int(arg[0])][2])
            else:
                half = UNITS[int(arg[0])][2] // 2
                product(int(arg[0]), int(arg[1]), half * int(arg[2]), half * (int(arg[2]) + 1))
